import numpy as np
import ml_dtypes


def mxq(x, axis, fmt="e4m3"):
    dtype, down = {"e4m3": (ml_dtypes.float8_e4m3fn, 7), "e5m2": (ml_dtypes.float8_e5m2, 14)}[fmt]
    v = np.moveaxis(np.asarray(x, np.float32).astype(ml_dtypes.bfloat16).astype(np.float64), axis, -1)
    blocks = v.reshape(v.shape[:-1] + (-1, 32))
    amax = np.abs(blocks).max(-1, keepdims=True)
    byte = np.maximum(np.where(amax > 0, np.frexp(amax)[1] - 1 + 127, 0) - down, 1)
    scale = np.exp2(byte - 127.0)
    codes = (blocks / scale).astype(np.float32).astype(dtype).astype(np.float64)
    return np.moveaxis((codes * scale).reshape(v.shape), -1, axis)


WIDE = False


def mx_kscale(k):
    if not WIDE:
        return np.ones(k)
    levels = np.array([10, -10, 5, -5, 0])
    if k % 512:
        return np.exp2(np.random.permutation(np.resize(levels, k // 32))).repeat(32)
    a = np.empty((k // 512, 16))
    for p in range(k // 512):
        a[p, :8] = np.random.permutation(np.resize(levels, 8))
        for g in range(8):
            far = levels[np.abs(levels - a[p, g]) >= 10]
            a[p, g + 8] = far[np.random.randint(len(far))]
    return np.exp2(a.ravel()).repeat(32)


def f64(x):
    return np.asarray(x).astype(np.float64)


def striped(idx):
    return np.tile(idx.reshape(-1, 16).T, (8, 1)).astype(np.uint16)


def unstriped(offs):
    return offs[:16].T.reshape(-1).astype(np.int64)


def relu2(v):
    return np.maximum(v, 0.0) ** 2


K, T, E, C, H, N = 512, 512, 4, 256, 1024, 384


def by_expert(wq, xq):
    return np.concatenate([wq[e].T @ xq[:, e * C:(e + 1) * C] for e in range(E)], axis=1)


def setup_inputs():
    n = np.random.standard_normal
    s = mx_kscale(K)[:, None]
    u = mx_kscale(H)
    first = np.random.permutation(np.repeat(np.arange(E), T // E))
    second = (first + 1 + np.random.permutation(np.repeat(np.arange(E - 1), -(-T // (E - 1)))[:T])) % E
    while np.bincount(second, minlength=E).max() != T // E:
        load = np.bincount(second, minlength=E); hi, lo = int(load.argmax()), int(load.argmin())
        t = np.flatnonzero((second == hi) & (first != lo))[0]; second[t] = lo
    slot_token = np.empty(E * C, np.int64); pos = np.empty((2, T), np.int64); fill = np.zeros(E, np.int64)
    place = np.stack([np.random.permutation(C) for _ in range(E)])
    for r, deal in enumerate((first, second)):
        for t in np.random.permutation(T):
            e = deal[t]; j = e * C + place[e, fill[e]]; fill[e] += 1; slot_token[j] = t; pos[r, t] = j
    g = np.random.uniform(0.2, 0.8, T)
    w_slot = np.empty(E * C); w_slot[pos[0]] = g; w_slot[pos[1]] = 1.0 - g
    return {
        "xT": (n((K, T)) * s).astype(np.float32),
        "w1": (n((E, K, H)) / np.sqrt(K) / s[None] * u[None, None, :]).astype(np.float32),
        "w2": (n((E, H, N)) / np.sqrt(H) / u[None, :, None] ** 2).astype(np.float32),
        "gate": np.tile(w_slot, (K, 1)).astype(np.float32),
        "offs": striped(slot_token),
        "pos1": striped(pos[0]),
        "pos2": striped(pos[1]),
    }


def reference(xT, w1, w2, gate, offs, pos1, pos2):
    idx = unstriped(offs)
    xq = mxq(f64(gate) * f64(xT)[:, idx], 0, "e4m3")
    h = relu2(by_expert(mxq(f64(w1), 1, "e4m3"), xq))
    y = by_expert(mxq(f64(w2), 1, "e4m3"), mxq(h, 0, "e4m3"))
    return y[:, unstriped(pos1)] + y[:, unstriped(pos2)]

@@ -1,0 +1,210 @@
+from contextlib import ExitStack
+
+import concourse.mybir as mybir
+
+K, T, E, C, H, N = 512, 512, 4, 256, 1024, 384
+S = E * C
+P = 128
+PACK = 4
+FLOPS = 2 * S * (K * H + H * N)
+BYTES = 4 * (K * T + E * K * H + E * H * N + P * S + N * T) + 2 * P * (S + 2 * T) // 16
+
+F32 = mybir.dt.float32
+BF16 = mybir.dt.bfloat16
+U32 = mybir.dt.uint32
+U16 = mybir.dt.uint16
+U8 = mybir.dt.uint8
+FP8X4 = mybir.dt.float8_e4m3fn_x4
+ACT = mybir.ActivationFunctionType
+ALU = mybir.AluOpType
+
+ORDER = "offs x0 g0 x1 x2 x3 g1 L0 L2 L4 L6 LA0 LA1 LA2 LA3 p1 p2 G00 G01 G02 G03 X0 QX0 c00 c01 LA4 LA5 LA6 LA7 Q00 Q01 M00 R00 M01 R01 S0 M10 R10 M11 R11 S1 G10 G11 G12 G13 X1 QX1 c20 c21 LB0 LB1 LB2 LB3 LB4 LB5 LB6 LB7 Q20 Q21 M20 R20 M21 R21 S2 M30 R30 M31 R31 S3 G20 G21 G22 G23 X2 QX2 c40 c41 Q40 Q41 M40 R40 M41 R41 S4 M50 R50 M51 R51 S5 G30 G31 G32 G33 c60 c61 Q60 H1 Q61 X3 H3 QX3 M60 R60 M61 R61 S6 M70 R70 M71 R71 S7 a0 a1 QA0 MA00 MA01 EA0 a2 a3 QA1 MA10 MA11 EA1 a4 a5 QA2 H5 H7 MA20 MA21 EA2 a6 a7 QA3 MA30 EA30 MA31 EA31 b0 QB0 MB0 EB0 b2 QB1 MB1 EB1 b4 QB2 MB2 EB2 b6 QB3 MB3 EB3 Y000 Y001 A00 ST00 Y100 Y101 A10 ST10 Y200 Y201 A20 ST20 Y210 Y211 A21 ST21".split()
+ON_SCALAR = "X0 X1 c00 c01 R00 R01 S0 R10 R11 S1 c20 R20 R21 S2 R30 R31 S3 R40 R41 S4 R50 R51 S5 R60 R61 S6 R70 R71 S7 EA0 b0 EB0 EA1 EB1 EA2 b4 EB2 EA30 b6 EB3".split()
+SPLIT = []
+WHOLE = 0
+SLOT = {"xb3":"w61","hc1":"w60","hc3":"xg3","hc5":"w20","hc7":"hb5","yg1":"r2","v2":"r0","vB":"r2","hf3":"hf0","hf4":"hf1","hf5":"hf2","hf6":"hf0","hf7":"hf1","wa0":"w00","ac0":"wc00","wb0":"xb0","wa1":"w01","ac1":"wc01","wb1":"xb1","wa2":"w20","ac2":"wc20","wb2":"xb2","wa3":"w21","ac3":"wc21","wb3":"w61","yg0":"xg0","yg2":"xg2"}
+
+
+def tile_moe_pre_mlp_relu2_kernel(tc, xT, w1, w2, gate, offs, pos1, pos2, out):
+    nc = tc.nc
+    with ExitStack() as ctx:
+        keep = ctx.enter_context(tc.tile_pool(name="keep", bufs=1))
+        sb = ctx.enter_context(tc.tile_pool(name="sb", bufs=1))
+        psum = ctx.enter_context(tc.psum_pool(name="psum", bufs=1))
+        tiles = {}
+
+        def tile(name, cols, dtype):
+            if name not in tiles:
+                tiles[name] = sb.tile([P, cols], dtype, name=name, tag=SLOT.get(name, name), bufs=1, align_bytes=64)
+            return tiles[name]
+
+        def cast(step, dst, src):
+            if step in ON_SCALAR:
+                nc.scalar.copy(dst, src)
+            else:
+                nc.vector.tensor_copy(dst, src)
+
+        def quantize(name, src):
+            cols = src.shape[1] // PACK
+            nc.vector.quantize_mx(
+                out=tile(name, cols, U32)[:].bitcast(FP8X4), scales=tile(name + "s", cols, U8)[:], in_=src[:]
+            )
+
+        def mm(dst, lname, lcols, rname, rcols, start, stop):
+            nc.tensor.matmul_mx(
+                out=dst,
+                lhsT=tiles[lname][:, lcols].bitcast(FP8X4),
+                lhsT_scale=tiles[lname + "s"][:, lcols],
+                rhs=tiles[rname][:, rcols].bitcast(FP8X4),
+                rhs_scale=tiles[rname + "s"][:, rcols],
+                start=start,
+                stop=stop,
+            )
+
+        offs_t = keep.tile([P, S // 16], U16, name="offs_t")
+        pos_t = [keep.tile([P, T // 16], U16, name="pos%d_t" % r) for r in range(2)]
+        x_rows = [keep.tile([P, T], F32, name="x_rows%d" % j) for j in range(PACK)]
+        gate_t = [keep.tile([P, C], F32, name="gate_first"), keep.tile([P, S - C], F32, name="gate_rest")]
+        y_a = keep.tile([P, 2, S], F32, name="y_a")
+        y_b = keep.tile([P, S], F32, name="y_b")
+        xT_v = xT.rearrange("(p j) t -> p j t", j=PACK)
+        gate_v = gate.rearrange("(p j) s -> p j s", j=PACK)
+        banks = {}
+
+        def w2_rows(u):
+            return w2[u // 2, (u % 2) * 512 : (u % 2 + 1) * 512, :].rearrange("(p j) n -> p j n", j=PACK)
+
+        def raw_a(u):
+            width = [N if v < WHOLE else 256 for v in range(8)]
+            group = [2 * (u // 2), 2 * (u // 2) + 1] if SPLIT or u < 4 else [4, 5, 6, 7]
+            lo = PACK * sum(width[v] for v in group if v < u)
+            t = tile("v%d" % (group[0] // 2), PACK * sum(width[v] for v in group), F32)
+            return t[:, lo : lo + PACK * width[u]].rearrange("p (j n) -> p j n", j=PACK)
+
+        def raw_b(e):
+            return tile("vB", 4096, F32)[:, e * 1024 : (e + 1) * 1024].rearrange("p (j n) -> p j n", j=PACK)
+
+        def inter(ap):
+            return ap.rearrange("p (c i j) -> p c j i", i=4, j=PACK)
+
+        def lines(ap):
+            return ap.rearrange("p j (c i) -> p c j i", i=4)
+
+        for step in ORDER:
+            kind = "".join([ch for ch in step if ch not in "0123456789"])
+            d = [int(ch) for ch in step if ch in "0123456789"]
+            if kind == "offs":
+                nc.sync.dma_start(offs_t[:], offs)
+            elif kind == "p":
+                nc.sync.dma_start(pos_t[d[0] - 1][:], pos1 if d[0] == 1 else pos2)
+            elif kind == "x":
+                nc.sync.dma_start(x_rows[d[0]][:], xT_v[:, d[0], :])
+            elif kind == "g":
+                nc.sync.dma_start(gate_t[d[0]][:], gate_v[:, 0, 0:C] if d[0] == 0 else gate_v[:, 0, C:S])
+            elif kind == "L":
+                u = d[0]
+                src = w1[u // 2].rearrange("(p j) h -> p j h", j=PACK)
+                if u // 2 in SPLIT:
+                    src = src[:, :, (u % 2) * 512 : (u % 2 + 1) * 512]
+                t = tile("r%d" % u, PACK * src.shape[2], F32)
+                nc.sync.dma_start(t[:].rearrange("p (j c) -> p j c", j=PACK), src)
+            elif kind == "LA":
+                nc.sync.dma_start(raw_a(d[0]), w2_rows(d[0]) if d[0] < WHOLE else w2_rows(d[0])[:, :, 0:256])
+            elif kind == "LB":
+                nc.sync.dma_start(raw_b(d[0] // 2)[:, :, (d[0] % 2) * P : (d[0] % 2 + 1) * P], w2_rows(d[0])[:, :, 256:384])
+            elif kind == "G":
+                e, j = d
+                gate_e = gate_t[0][:] if e == 0 else gate_t[1][:, (e - 1) * C : e * C]
+                nc.vector.tensor_tensor(
+                    tile("xg%d" % e, PACK * C, F32)[:, j * C : (j + 1) * C],
+                    x_rows[j][:].indirect(offs_t[:, e * 16 : (e + 1) * 16]),
+                    gate_e,
+                    ALU.mult,
+                )
+            elif kind == "X":
+                e = d[0]
+                src = tiles["xg%d" % e][:].rearrange("p (j c) -> p j c", j=PACK)
+                cast(step, inter(tile("xb%d" % e, PACK * C, BF16)[:]), lines(src))
+            elif kind == "QX":
+                quantize("xc%d" % d[0], tiles["xb%d" % d[0]])
+            elif kind == "c":
+                u, h = d
+                dst = tile("w%d%d" % (u, h), 2048, BF16)[:].rearrange("p (t m j) -> p m j t", t=2, j=PACK)
+                src = tiles["r%d" % u][:].rearrange("p (j m t) -> p m j t", j=PACK, t=PACK)[:, :, :, 2 * h : 2 * h + 2]
+                cast(step, dst, src)
+            elif kind == "Q":
+                quantize("wc%d%d" % (d[0], d[1]), tiles["w%d%d" % (d[0], d[1])])
+            elif kind == "M":
+                u, s = d
+                banks[step] = psum.tile([P, PACK, P], F32, name="a%d%d" % (u, s), tag="bank", bufs=8)
+                for t in range(PACK):
+                    mm(
+                        banks[step][:, t, :],
+                        "wc%d%d" % (u // 2 * 2, t // 2),
+                        slice((t % 2) * 256 + (u % 2) * P, (t % 2) * 256 + (u % 2 + 1) * P),
+                        "xc%d" % (u // 2),
+                        slice(s * P, (s + 1) * P),
+                        True,
+                        True,
+                    )
+            elif kind == "R":
+                u, s = d
+                dst = tile("hf%d" % u, 1024, F32)[:, s * 512 : (s + 1) * 512].rearrange("p (n t) -> p n t", t=PACK)
+                src = banks["M%d%d" % (u, s)][:].rearrange("p t n -> p n t")
+                if step in ON_SCALAR:
+                    nc.scalar.activation(dst, src, ACT.Relu)
+                else:
+                    nc.vector.tensor_scalar_max(dst, src, 0.0)
+            elif kind == "S":
+                u = d[0]
+                dst = tile("hb%d" % (u // 2 * 2 + 1), 2048, BF16)[:, (u % 2) * 1024 : (u % 2 + 1) * 1024]
+                nc.scalar.activation(dst, tiles["hf%d" % u][:], ACT.Square)
+            elif kind == "H":
+                quantize("hc%d" % d[0], tiles["hb%d" % d[0]])
+            elif kind == "a":
+                u = d[0]
+                dst = tile("wa%d" % (u // 2), 2048, BF16)[:, (u % 2) * 1024 : (u % 2 + 1) * 1024]
+                cast(step, inter(dst), lines(raw_a(u)))
+            elif kind == "QA":
+                quantize("ac%d" % d[0], tiles["wa%d" % d[0]])
+            elif kind == "MA":
+                e, i = d
+                key = "A%d" % e if e < 3 else "A3%d" % i
+                if key not in banks:
+                    banks[key] = psum.tile([P, 2, C], F32, name="y" + key, tag="bank", bufs=8)
+                for g in range(2):
+                    cols = slice(g * 256 + i * P, g * 256 + (i + 1) * P)
+                    mm(banks[key][:, i, :], "ac%d" % e, cols, "hc%d" % (2 * e + 1), slice(g * C, (g + 1) * C), g == 0, g == 1)
+            elif kind == "EA":
+                e = d[0]
+                if e < 3:
+                    cast(step, y_a[:, :, e * C : (e + 1) * C], banks["A%d" % e][:])
+                else:
+                    cast(step, y_a[:, d[1], e * C : (e + 1) * C], banks["A3%d" % d[1]][:, d[1], :])
+            elif kind == "b":
+                e = d[0] // 2
+                cast(step, inter(tile("wb%d" % e, 1024, BF16)[:]), lines(raw_b(e)))
+            elif kind == "QB":
+                quantize("bc%d" % d[0], tiles["wb%d" % d[0]])
+            elif kind == "MB":
+                e = d[0]
+                banks[step] = psum.tile([P, C], F32, name="yB%d" % e, tag="bank", bufs=8)
+                for g in range(2):
+                    mm(banks[step][:], "bc%d" % e, slice(g * P, (g + 1) * P), "hc%d" % (2 * e + 1), slice(g * C, (g + 1) * C), g == 0, g == 1)
+            elif kind == "EB":
+                e = d[0]
+                cast(step, y_b[:, e * C : (e + 1) * C], banks["MB%d" % e][:])
+            else:
+                i, q = d[0], d[1]
+                lo, hi = ((0, 384), (384, T))[q] if i == 2 else (0, T)
+                yg = tile("yg%d" % i, 2 * T, F32)
+                first = yg[:, lo:hi]
+                second = yg[:, T + lo : T + hi]
+                total = first
+                if kind == "Y":
+                    window = y_a[:, i, :] if i < 2 else y_b[:]
+                    nc.vector.tensor_copy(second if d[2] else first, window.indirect(pos_t[d[2]][:, lo // 16 : hi // 16]))
+                elif kind == "A":
+                    nc.vector.tensor_add(total, first, second)
+                else:
+                    nc.sync.dma_start(out[i * P : (i + 1) * P, lo:hi], total)

@@ -22,7 +22,7 @@ ORDER = "offs x0 g0 x1 x2 x3 g1 L0 L2 L4 L6 LA0 LA1 LA2 LA3 p1 p2 G00 G01 G02 G0
 ON_SCALAR = "X0 X1 c00 c01 R00 R01 S0 R10 R11 S1 c20 R20 R21 S2 R30 R31 S3 R40 R41 S4 R50 R51 S5 R60 R61 S6 R70 R71 S7 EA0 b0 EB0 EA1 EB1 EA2 b4 EB2 EA30 b6 EB3".split()
 SPLIT = []
 WHOLE = 0
-SLOT = {"xb3":"w61","hc1":"w60","hc3":"xg3","hc5":"w20","hc7":"hb5","yg1":"r2","v2":"r0","vB":"r2","hf3":"hf0","hf4":"hf1","hf5":"hf2","hf6":"hf0","hf7":"hf1","wa0":"w00","ac0":"wc00","wb0":"xb0","wa1":"w01","ac1":"wc01","wb1":"xb1","wa2":"w20","ac2":"wc20","wb2":"xb2","wa3":"w21","ac3":"wc21","wb3":"w61","yg0":"xg0","yg2":"xg2"}
+SLOT = {"xb3":"w61","hc1":"w60","hc3":"xg3","hc5":"w20","hc7":"hb5","o0":"w61","yg1":"r2","v2":"r0","vB":"r2","hf3":"hf0","hf4":"hf1","hf5":"hf2","hf6":"hf0","hf7":"hf1","wa0":"w00","ac0":"wc00","wb0":"xb0","wa1":"w01","ac1":"wc01","wb1":"xb1","wa2":"w20","ac2":"wc20","wb2":"xb2","wa3":"w21","ac3":"wc21","wb3":"w61","yg0":"xg0","yg2":"xg2"}
 
 
 def tile_moe_pre_mlp_relu2_kernel(tc, xT, w1, w2, gate, offs, pos1, pos2, out):
@@ -200,11 +200,11 @@ def tile_moe_pre_mlp_relu2_kernel(tc, xT, w1, w2, gate, offs, pos1, pos2, out):
                 yg = tile("yg%d" % i, 2 * T, F32)
                 first = yg[:, lo:hi]
                 second = yg[:, T + lo : T + hi]
-                total = first
+                total = tile("o%d" % i, T, F32)[:] if i < 2 and kind != "Y" else first
                 if kind == "Y":
                     window = y_a[:, i, :] if i < 2 else y_b[:]
                     nc.vector.tensor_copy(second if d[2] else first, window.indirect(pos_t[d[2]][:, lo // 16 : hi // 16]))
                 elif kind == "A":
-                    nc.vector.tensor_add(total, first, second)
+                    (nc.gpsimd if i < 2 else nc.vector).tensor_add(total, first, second)
                 else:
                     nc.sync.dma_start(out[i * P : (i + 1) * P, lo:hi], total)

@@ -6,8 +6,22 @@ K, T, E, C, H, N = 512, 512, 4, 256, 1024, 384
 S = E * C
 P = 128
 PACK = 4
+PASS = P * PACK
+G = H // PASS
+PER_COL = 16
 FLOPS = 2 * S * (K * H + H * N)
-BYTES = 4 * (K * T + E * K * H + E * H * N + P * S + N * T) + 2 * P * (S + 2 * T) // 16
+BYTES = 4 * (K * T + E * K * H + E * H * N + P * S + N * T) + 2 * P * (S + 2 * T) // PER_COL
+
+GROUPS = ((0,), (1,), (2, 3))
+WINDOW = T + PER_COL
+FRONT = 2 * P
+BACK = N - FRONT
+LAST = E - 1
+RELU_RING = 3
+
+X_ON_SCALAR = (0, 1)
+W1_ON_SCALAR = ((0, 0), (0, 1), (1, 1))
+BACK_ON_SCALAR = (1, 3)
 
 F32 = mybir.dt.float32
 BF16 = mybir.dt.bfloat16
@@ -18,193 +32,220 @@ FP8X4 = mybir.dt.float8_e4m3fn_x4
 ACT = mybir.ActivationFunctionType
 ALU = mybir.AluOpType
 
-ORDER = "offs x0 g0 x1 x2 x3 g1 L0 L2 L4 L6 LA0 LA1 LA2 LA3 p1 p2 G00 G01 G02 G03 X0 QX0 c00 c01 LA4 LA5 LA6 LA7 Q00 Q01 M00 R00 M01 R01 S0 M10 R10 M11 R11 S1 G10 G11 G12 G13 X1 QX1 c20 c21 LB0 LB1 LB2 LB3 LB4 LB5 LB6 LB7 Q20 Q21 M20 R20 M21 R21 S2 M30 R30 M31 R31 S3 G20 G21 G22 G23 X2 QX2 c40 c41 Q40 Q41 M40 R40 M41 R41 S4 M50 R50 M51 R51 S5 G30 G31 G32 G33 c60 c61 Q60 H1 Q61 X3 H3 QX3 M60 R60 M61 R61 S6 M70 R70 M71 R71 S7 a0 a1 QA0 MA00 MA01 EA0 a2 a3 QA1 MA10 MA11 EA1 a4 a5 QA2 H5 H7 MA20 MA21 EA2 a6 a7 QA3 MA30 EA30 MA31 EA31 b0 QB0 MB0 EB0 b2 QB1 MB1 EB1 b4 QB2 MB2 EB2 b6 QB3 MB3 EB3 Y000 Y001 A00 ST00 Y100 Y101 A10 ST10 Y200 Y201 A20 ST20 Y210 Y211 A21 ST21".split()
-ON_SCALAR = "X0 X1 c00 c01 R00 R01 S0 R10 R11 S1 c20 R20 R21 S2 R30 R31 S3 R40 R41 S4 R50 R51 S5 R60 R61 S6 R70 R71 S7 EA0 b0 EB0 EA1 EB1 EA2 b4 EB2 EA30 b6 EB3".split()
-SPLIT = []
-WHOLE = 0
-SLOT = {"xb3":"w61","hc1":"w60","hc3":"xg3","hc5":"w20","hc7":"hb5","o0":"w61","yg1":"r2","v2":"r0","vB":"r2","hf3":"hf0","hf4":"hf1","hf5":"hf2","hf6":"hf0","hf7":"hf1","wa0":"w00","ac0":"wc00","wb0":"xb0","wa1":"w01","ac1":"wc01","wb1":"xb1","wa2":"w20","ac2":"wc20","wb2":"xb2","wa3":"w21","ac3":"wc21","wb3":"w61","yg0":"xg0","yg2":"xg2"}
-
 
 def tile_moe_pre_mlp_relu2_kernel(tc, xT, w1, w2, gate, offs, pos1, pos2, out):
     nc = tc.nc
     with ExitStack() as ctx:
         keep = ctx.enter_context(tc.tile_pool(name="keep", bufs=1))
-        sb = ctx.enter_context(tc.tile_pool(name="sb", bufs=1))
+        work = ctx.enter_context(tc.tile_pool(name="work", bufs=1))
         psum = ctx.enter_context(tc.psum_pool(name="psum", bufs=1))
-        tiles = {}
 
-        def tile(name, cols, dtype):
-            if name not in tiles:
-                tiles[name] = sb.tile([P, cols], dtype, name=name, tag=SLOT.get(name, name), bufs=1, align_bytes=64)
-            return tiles[name]
+        def new(name, cols, dtype, on=None):
+            return work.tile([P, cols], dtype, name=name, tag=on or name, bufs=1, align_bytes=64)
 
-        def cast(step, dst, src):
-            if step in ON_SCALAR:
+        def new_bank(name, shape):
+            return psum.tile(shape, F32, name=name, tag="bank", bufs=8)
+
+        def copy(on_scalar, dst, src):
+            if on_scalar:
                 nc.scalar.copy(dst, src)
             else:
                 nc.vector.tensor_copy(dst, src)
 
-        def quantize(name, src):
-            cols = src.shape[1] // PACK
-            nc.vector.quantize_mx(
-                out=tile(name, cols, U32)[:].bitcast(FP8X4), scales=tile(name + "s", cols, U8)[:], in_=src[:]
+        def interleave(on_scalar, dst, rows):
+            copy(
+                on_scalar,
+                dst.rearrange("p (c i j) -> p c j i", i=4, j=PACK),
+                rows.rearrange("p j (c i) -> p c j i", i=4),
             )
 
-        def mm(dst, lname, lcols, rname, rcols, start, stop):
+        def quantize(name, src, on=None):
+            cols = src.shape[1] // PACK
+            words = new(name, cols, U32, on)
+            scales = new(name + "_scales", cols, U8)
+            nc.vector.quantize_mx(out=words[:].bitcast(FP8X4), scales=scales[:], in_=src[:])
+            return words, scales
+
+        def matmul(dst, lhs, lhs_col, rhs, rhs_col, width, start, stop):
+            lcols = slice(lhs_col, lhs_col + P)
+            rcols = slice(rhs_col, rhs_col + width)
             nc.tensor.matmul_mx(
                 out=dst,
-                lhsT=tiles[lname][:, lcols].bitcast(FP8X4),
-                lhsT_scale=tiles[lname + "s"][:, lcols],
-                rhs=tiles[rname][:, rcols].bitcast(FP8X4),
-                rhs_scale=tiles[rname + "s"][:, rcols],
+                lhsT=lhs[0][:, lcols].bitcast(FP8X4),
+                lhsT_scale=lhs[1][:, lcols],
+                rhs=rhs[0][:, rcols].bitcast(FP8X4),
+                rhs_scale=rhs[1][:, rcols],
                 start=start,
                 stop=stop,
             )
 
-        offs_t = keep.tile([P, S // 16], U16, name="offs_t")
-        pos_t = [keep.tile([P, T // 16], U16, name="pos%d_t" % r) for r in range(2)]
-        x_rows = [keep.tile([P, T], F32, name="x_rows%d" % j) for j in range(PACK)]
-        gate_t = [keep.tile([P, C], F32, name="gate_first"), keep.tile([P, S - C], F32, name="gate_rest")]
-        y_a = keep.tile([P, 2, S], F32, name="y_a")
-        y_b = keep.tile([P, S], F32, name="y_b")
-        xT_v = xT.rearrange("(p j) t -> p j t", j=PACK)
-        gate_v = gate.rearrange("(p j) s -> p j s", j=PACK)
-        banks = {}
+        def by_row(ap):
+            return ap.rearrange("p (j c) -> p j c", j=PACK)
 
-        def w2_rows(u):
-            return w2[u // 2, (u % 2) * 512 : (u % 2 + 1) * 512, :].rearrange("(p j) n -> p j n", j=PACK)
+        def w2_pass(e, g):
+            return w2[e, g * PASS : (g + 1) * PASS, :].rearrange("(p j) n -> p j n", j=PACK)
 
-        def raw_a(u):
-            width = [N if v < WHOLE else 256 for v in range(8)]
-            group = [2 * (u // 2), 2 * (u // 2) + 1] if SPLIT or u < 4 else [4, 5, 6, 7]
-            lo = PACK * sum(width[v] for v in group if v < u)
-            t = tile("v%d" % (group[0] // 2), PACK * sum(width[v] for v in group), F32)
-            return t[:, lo : lo + PACK * width[u]].rearrange("p (j n) -> p j n", j=PACK)
+        offs_list = keep.tile([P, S // PER_COL], U16, name="offs_list")
+        pos_lists = [keep.tile([P, T // PER_COL], U16, name="pos_list%d" % r) for r in range(2)]
+        tokens = [keep.tile([P, WINDOW], F32, name="tokens%d" % j) for j in range(PACK)]
+        gate_first = keep.tile([P, C], F32, name="gate_first")
+        gate_rest = keep.tile([P, S - C], F32, name="gate_rest")
+        y_front = keep.tile([P, FRONT // P, S], F32, name="y_front")
+        y_back = keep.tile([P, S], F32, name="y_back")
 
-        def raw_b(e):
-            return tile("vB", 4096, F32)[:, e * 1024 : (e + 1) * 1024].rearrange("p (j n) -> p j n", j=PACK)
+        for j in range(PACK):
+            nc.gpsimd.memset(tokens[j][:, T:WINDOW], 0.0)
 
-        def inter(ap):
-            return ap.rearrange("p (c i j) -> p c j i", i=4, j=PACK)
+        xT_rows = xT.rearrange("(p j) t -> p j t", j=PACK)
+        gate_row = gate.rearrange("(p j) s -> p j s", j=PACK)[:, 0, :]
+        nc.sync.dma_start(offs_list[:], offs)
+        nc.sync.dma_start(tokens[0][:, 0:T], xT_rows[:, 0, :])
+        nc.sync.dma_start(gate_first[:], gate_row[:, 0:C])
+        for j in range(1, PACK):
+            nc.sync.dma_start(tokens[j][:, 0:T], xT_rows[:, j, :])
+        nc.sync.dma_start(gate_rest[:], gate_row[:, C:S])
+        w1_raw = []
+        for e in range(E):
+            w1_raw.append(new("w1_raw%d" % e, PACK * H, F32))
+            nc.sync.dma_start(by_row(w1_raw[e][:]), w1[e].rearrange("(p j) i -> p j i", j=PACK))
 
-        def lines(ap):
-            return ap.rearrange("p j (c i) -> p c j i", i=4)
+        w2_whole = new("w2_whole", G * PACK * N, F32)
+        whole = [by_row(w2_whole[:, g * PACK * N : (g + 1) * PACK * N]) for g in range(G)]
+        for g in range(G):
+            nc.sync.dma_start(whole[g], w2_pass(0, g))
+        front_raw, back_raw = {}, {}
 
-        for step in ORDER:
-            kind = "".join([ch for ch in step if ch not in "0123456789"])
-            d = [int(ch) for ch in step if ch in "0123456789"]
-            if kind == "offs":
-                nc.sync.dma_start(offs_t[:], offs)
-            elif kind == "p":
-                nc.sync.dma_start(pos_t[d[0] - 1][:], pos1 if d[0] == 1 else pos2)
-            elif kind == "x":
-                nc.sync.dma_start(x_rows[d[0]][:], xT_v[:, d[0], :])
-            elif kind == "g":
-                nc.sync.dma_start(gate_t[d[0]][:], gate_v[:, 0, 0:C] if d[0] == 0 else gate_v[:, 0, C:S])
-            elif kind == "L":
-                u = d[0]
-                src = w1[u // 2].rearrange("(p j) h -> p j h", j=PACK)
-                if u // 2 in SPLIT:
-                    src = src[:, :, (u % 2) * 512 : (u % 2 + 1) * 512]
-                t = tile("r%d" % u, PACK * src.shape[2], F32)
-                nc.sync.dma_start(t[:].rearrange("p (j c) -> p j c", j=PACK), src)
-            elif kind == "LA":
-                nc.sync.dma_start(raw_a(d[0]), w2_rows(d[0]) if d[0] < WHOLE else w2_rows(d[0])[:, :, 0:256])
-            elif kind == "LB":
-                nc.sync.dma_start(raw_b(d[0] // 2)[:, :, (d[0] % 2) * P : (d[0] % 2 + 1) * P], w2_rows(d[0])[:, :, 256:384])
-            elif kind == "G":
-                e, j = d
-                gate_e = gate_t[0][:] if e == 0 else gate_t[1][:, (e - 1) * C : e * C]
+        def load_w2_part(raw, name, experts, first_col, width, on=None):
+            size = PACK * G * width
+            held = new(name, len(experts) * size, F32, on)
+            for place, e in enumerate(experts):
+                raw[e] = by_row(held[:, place * size : (place + 1) * size])
+                for g in range(G):
+                    src = w2_pass(e, g)[:, :, first_col : first_col + width]
+                    nc.sync.dma_start(raw[e][:, :, g * width : (g + 1) * width], src)
+
+        load_w2_part(front_raw, "front_raw1", (1,), 0, FRONT)
+        nc.sync.dma_start(pos_lists[0][:], pos1)
+        nc.sync.dma_start(pos_lists[1][:], pos2)
+
+        def gather_group(q):
+            lo, hi = GROUPS[q][0] * C, (GROUPS[q][-1] + 1) * C
+            gathered = new("gathered%d" % q, PACK * (hi - lo), F32)
+            for j in range(PACK):
                 nc.vector.tensor_tensor(
-                    tile("xg%d" % e, PACK * C, F32)[:, j * C : (j + 1) * C],
-                    x_rows[j][:].indirect(offs_t[:, e * 16 : (e + 1) * 16]),
-                    gate_e,
+                    by_row(gathered[:])[:, j, :],
+                    tokens[j][:].indirect(offs_list[:, lo // PER_COL : hi // PER_COL]),
+                    gate_first[:] if q == 0 else gate_rest[:, lo - C : hi - C],
                     ALU.mult,
                 )
-            elif kind == "X":
-                e = d[0]
-                src = tiles["xg%d" % e][:].rearrange("p (j c) -> p j c", j=PACK)
-                cast(step, inter(tile("xb%d" % e, PACK * C, BF16)[:]), lines(src))
-            elif kind == "QX":
-                quantize("xc%d" % d[0], tiles["xb%d" % d[0]])
-            elif kind == "c":
-                u, h = d
-                dst = tile("w%d%d" % (u, h), 2048, BF16)[:].rearrange("p (t m j) -> p m j t", t=2, j=PACK)
-                src = tiles["r%d" % u][:].rearrange("p (j m t) -> p m j t", j=PACK, t=PACK)[:, :, :, 2 * h : 2 * h + 2]
-                cast(step, dst, src)
-            elif kind == "Q":
-                quantize("wc%d%d" % (d[0], d[1]), tiles["w%d%d" % (d[0], d[1])])
-            elif kind == "M":
-                u, s = d
-                banks[step] = psum.tile([P, PACK, P], F32, name="a%d%d" % (u, s), tag="bank", bufs=8)
-                for t in range(PACK):
-                    mm(
-                        banks[step][:, t, :],
-                        "wc%d%d" % (u // 2 * 2, t // 2),
-                        slice((t % 2) * 256 + (u % 2) * P, (t % 2) * 256 + (u % 2 + 1) * P),
-                        "xc%d" % (u // 2),
-                        slice(s * P, (s + 1) * P),
-                        True,
-                        True,
+            rounded = new("x_bf%d" % q, PACK * (hi - lo), BF16)
+            interleave(q in X_ON_SCALAR, rounded[:], by_row(gathered[:]))
+            return quantize("x_words%d" % q, rounded, "w1_bf0_1" if q == len(GROUPS) - 1 else None)
+
+        h_words_on = ("w1_bf3_0", "w1_bf3_1", "w1_bf1_0", "h_bf2")
+        h_bf, h_words = {}, {}
+
+        def quantize_h(e):
+            h_words[e] = quantize("h_words%d" % e, h_bf[e], h_words_on[e])
+
+        x_words = {}
+        for e in range(E):
+            for q, group in enumerate(GROUPS):
+                if e == group[0]:
+                    group_words = gather_group(q)
+                    for place, member in enumerate(group):
+                        x_words[member] = (group_words, place * C)
+            halves = []
+            for a in range(2):
+                halves.append(new("w1_bf%d_%d" % (e, a), 2 * PACK * G * P, BF16))
+                copy(
+                    (e, a) in W1_ON_SCALAR,
+                    halves[a][:].rearrange("p (t m j) -> p m j t", t=2, j=PACK),
+                    w1_raw[e][:].rearrange("p (j m t) -> p m j t", j=PACK, t=PACK)[:, :, :, 2 * a : 2 * a + 2],
+                )
+            if e == 0:
+                load_w2_part(front_raw, "front_raw23", (2, 3), 0, FRONT, "w1_raw0")
+            if e == 1:
+                load_w2_part(back_raw, "back_raw", (1, 2, 3), FRONT, BACK, "w1_raw1")
+            w1_words = []
+            for a in range(2):
+                w1_words.append(quantize("w1_words%d_%d" % (e, a), halves[a]))
+                if e == LAST:
+                    quantize_h(a)
+            for g in range(G):
+                relu = new("relu%d_%d" % (e, g), PACK * C, F32, "relu_ring%d" % ((G * e + g) % RELU_RING))
+                for s in range(C // P):
+                    bank = new_bank("a%d_%d_%d" % (e, g, s), [P, PACK, P])
+                    for t in range(PACK):
+                        col = (t % 2) * G * P + g * P
+                        matmul(bank[:, t, :], w1_words[t // 2], col, x_words[e][0], x_words[e][1] + s * P, P, True, True)
+                    nc.scalar.activation(
+                        relu[:, s * PASS : (s + 1) * PASS].rearrange("p (n t) -> p n t", t=PACK),
+                        bank[:].rearrange("p t n -> p n t"),
+                        ACT.Relu,
                     )
-            elif kind == "R":
-                u, s = d
-                dst = tile("hf%d" % u, 1024, F32)[:, s * 512 : (s + 1) * 512].rearrange("p (n t) -> p n t", t=PACK)
-                src = banks["M%d%d" % (u, s)][:].rearrange("p t n -> p n t")
-                if step in ON_SCALAR:
-                    nc.scalar.activation(dst, src, ACT.Relu)
-                else:
-                    nc.vector.tensor_scalar_max(dst, src, 0.0)
-            elif kind == "S":
-                u = d[0]
-                dst = tile("hb%d" % (u // 2 * 2 + 1), 2048, BF16)[:, (u % 2) * 1024 : (u % 2 + 1) * 1024]
-                nc.scalar.activation(dst, tiles["hf%d" % u][:], ACT.Square)
-            elif kind == "H":
-                quantize("hc%d" % d[0], tiles["hb%d" % d[0]])
-            elif kind == "a":
-                u = d[0]
-                dst = tile("wa%d" % (u // 2), 2048, BF16)[:, (u % 2) * 1024 : (u % 2 + 1) * 1024]
-                cast(step, inter(dst), lines(raw_a(u)))
-            elif kind == "QA":
-                quantize("ac%d" % d[0], tiles["wa%d" % d[0]])
-            elif kind == "MA":
-                e, i = d
-                key = "A%d" % e if e < 3 else "A3%d" % i
-                if key not in banks:
-                    banks[key] = psum.tile([P, 2, C], F32, name="y" + key, tag="bank", bufs=8)
-                for g in range(2):
-                    cols = slice(g * 256 + i * P, g * 256 + (i + 1) * P)
-                    mm(banks[key][:, i, :], "ac%d" % e, cols, "hc%d" % (2 * e + 1), slice(g * C, (g + 1) * C), g == 0, g == 1)
-            elif kind == "EA":
-                e = d[0]
-                if e < 3:
-                    cast(step, y_a[:, :, e * C : (e + 1) * C], banks["A%d" % e][:])
-                else:
-                    cast(step, y_a[:, d[1], e * C : (e + 1) * C], banks["A3%d" % d[1]][:, d[1], :])
-            elif kind == "b":
-                e = d[0] // 2
-                cast(step, inter(tile("wb%d" % e, 1024, BF16)[:]), lines(raw_b(e)))
-            elif kind == "QB":
-                quantize("bc%d" % d[0], tiles["wb%d" % d[0]])
-            elif kind == "MB":
-                e = d[0]
-                banks[step] = psum.tile([P, C], F32, name="yB%d" % e, tag="bank", bufs=8)
-                for g in range(2):
-                    mm(banks[step][:], "bc%d" % e, slice(g * P, (g + 1) * P), "hc%d" % (2 * e + 1), slice(g * C, (g + 1) * C), g == 0, g == 1)
-            elif kind == "EB":
-                e = d[0]
-                cast(step, y_b[:, e * C : (e + 1) * C], banks["MB%d" % e][:])
+                if g == 0:
+                    h_bf[e] = new("h_bf%d" % e, G * PACK * C, BF16)
+                nc.scalar.activation(h_bf[e][:, g * PACK * C : (g + 1) * PACK * C], relu[:], ACT.Square)
+
+        def second_layer(dst, w2_words, width, block, e):
+            for g in range(G):
+                matmul(dst, w2_words, g * width + block * P, h_words[e], g * C, C, g == 0, g == G - 1)
+
+        front_bf_on = ("w1_bf0_0", None, "w1_bf1_0", "w1_bf1_1")
+        for e in range(E):
+            rounded = new("front_bf%d" % e, G * PACK * FRONT, BF16, front_bf_on[e])
+            if e in (0, LAST):
+                for g in range(G):
+                    rows = whole[g][:, :, 0:FRONT] if e == 0 else front_raw[e][:, :, g * FRONT : (g + 1) * FRONT]
+                    interleave(False, rounded[:, g * PACK * FRONT : (g + 1) * PACK * FRONT], rows)
             else:
-                i, q = d[0], d[1]
-                lo, hi = ((0, 384), (384, T))[q] if i == 2 else (0, T)
-                yg = tile("yg%d" % i, 2 * T, F32)
-                first = yg[:, lo:hi]
-                second = yg[:, T + lo : T + hi]
-                total = tile("o%d" % i, T, F32)[:] if i < 2 and kind != "Y" else first
-                if kind == "Y":
-                    window = y_a[:, i, :] if i < 2 else y_b[:]
-                    nc.vector.tensor_copy(second if d[2] else first, window.indirect(pos_t[d[2]][:, lo // 16 : hi // 16]))
-                elif kind == "A":
-                    (nc.gpsimd if i < 2 else nc.vector).tensor_add(total, first, second)
-                else:
-                    nc.sync.dma_start(out[i * P : (i + 1) * P, lo:hi], total)
+                interleave(False, rounded[:], front_raw[e])
+            words = quantize("front_words%d" % e, rounded, "w1_words%d_%d" % divmod(e, 2))
+            if e == LAST - 1:
+                quantize_h(e)
+                quantize_h(LAST)
+            slots = slice(e * C, (e + 1) * C)
+            if e < LAST:
+                bank = new_bank("y_front%d" % e, [P, FRONT // P, C])
+                for block in range(FRONT // P):
+                    second_layer(bank[:, block, :], words, FRONT, block, e)
+                nc.scalar.copy(y_front[:, :, slots], bank[:])
+            else:
+                for block in range(FRONT // P):
+                    bank = new_bank("y_front%d_%d" % (e, block), [P, FRONT // P, C])
+                    second_layer(bank[:, block, :], words, FRONT, block, e)
+                    nc.scalar.copy(y_front[:, block, slots], bank[:, block, :])
+
+        for e in range(E):
+            rounded = new("back_bf%d" % e, G * PACK * BACK, BF16, "x_bf%d" % e if e < len(GROUPS) else None)
+            if e == 0:
+                for g in range(G):
+                    interleave(False, rounded[:, g * PACK * BACK : (g + 1) * PACK * BACK], whole[g][:, :, FRONT:N])
+            else:
+                interleave(e in BACK_ON_SCALAR, rounded[:], back_raw[e])
+            words = quantize("back_words%d" % e, rounded)
+            bank = new_bank("y_back%d" % e, [P, C])
+            second_layer(bank[:], words, BACK, 0, e)
+            nc.scalar.copy(y_back[:, e * C : (e + 1) * C], bank[:])
+
+        def gather_results(picked, window, lo, hi):
+            pair = [picked[:, r * T + lo : r * T + hi] for r in range(2)]
+            for r in range(2):
+                nc.vector.tensor_copy(pair[r], window.indirect(pos_lists[r][:, lo // PER_COL : hi // PER_COL]))
+            return pair
+
+        picked_on = ("gathered0", "w1_raw1")
+        total_on = ("back_bf%d" % LAST, None)
+        for block in range(FRONT // P):
+            picked = new("picked%d" % block, 2 * T, F32, picked_on[block])
+            first, second = gather_results(picked, y_front[:, block, :], 0, T)
+            total = new("total%d" % block, T, F32, total_on[block])
+            nc.gpsimd.tensor_add(total[:], first, second)
+            nc.sync.dma_start(out[block * P : (block + 1) * P, :], total[:])
+
+        picked = new("picked_back", 2 * T, F32, "gathered%d" % (len(GROUPS) - 1))
+        for lo in range(0, T, T // 2):
+            first, second = gather_results(picked, y_back[:], lo, lo + T // 2)
+            nc.vector.tensor_add(first, first, second)
+            nc.sync.dma_start(out[FRONT:N, lo : lo + T // 2], first)

from contextlib import ExitStack

import concourse.mybir as mybir

K, T, E, C, H, N = 512, 512, 4, 256, 1024, 384
S = E * C
P = 128
PACK = 4
PASS = P * PACK
G = H // PASS
PER_COL = 16
FLOPS = 2 * S * (K * H + H * N)
BYTES = 4 * (K * T + E * K * H + E * H * N + P * S + N * T) + 2 * P * (S + 2 * T) // PER_COL

GROUPS = ((0,), (1,), (2, 3))
WINDOW = T + PER_COL
FRONT = 2 * P
BACK = N - FRONT
LAST = E - 1
RELU_RING = 3

X_ON_SCALAR = (0, 1)
W1_ON_SCALAR = ((0, 0), (0, 1), (1, 1))
BACK_ON_SCALAR = (1, 3)

F32 = mybir.dt.float32
BF16 = mybir.dt.bfloat16
U32 = mybir.dt.uint32
U16 = mybir.dt.uint16
U8 = mybir.dt.uint8
FP8X4 = mybir.dt.float8_e4m3fn_x4
ACT = mybir.ActivationFunctionType
ALU = mybir.AluOpType


def tile_moe_pre_mlp_relu2_kernel(tc, xT, w1, w2, gate, offs, pos1, pos2, out):
    nc = tc.nc
    with ExitStack() as ctx:
        keep = ctx.enter_context(tc.tile_pool(name="keep", bufs=1))
        work = ctx.enter_context(tc.tile_pool(name="work", bufs=1))
        psum = ctx.enter_context(tc.psum_pool(name="psum", bufs=1))

        def new(name, cols, dtype, on=None):
            return work.tile([P, cols], dtype, name=name, tag=on or name, bufs=1, align_bytes=64)

        def new_bank(name, shape):
            return psum.tile(shape, F32, name=name, tag="bank", bufs=8)

        def copy(on_scalar, dst, src):
            if on_scalar:
                nc.scalar.copy(dst, src)
            else:
                nc.vector.tensor_copy(dst, src)

        def interleave(on_scalar, dst, rows):
            copy(
                on_scalar,
                dst.rearrange("p (c i j) -> p c j i", i=4, j=PACK),
                rows.rearrange("p j (c i) -> p c j i", i=4),
            )

        def quantize(name, src, on=None):
            cols = src.shape[1] // PACK
            words = new(name, cols, U32, on)
            scales = new(name + "_scales", cols, U8)
            nc.vector.quantize_mx(out=words[:].bitcast(FP8X4), scales=scales[:], in_=src[:])
            return words, scales

        def matmul(dst, lhs, lhs_col, rhs, rhs_col, width, start, stop):
            lcols = slice(lhs_col, lhs_col + P)
            rcols = slice(rhs_col, rhs_col + width)
            nc.tensor.matmul_mx(
                out=dst,
                lhsT=lhs[0][:, lcols].bitcast(FP8X4),
                lhsT_scale=lhs[1][:, lcols],
                rhs=rhs[0][:, rcols].bitcast(FP8X4),
                rhs_scale=rhs[1][:, rcols],
                start=start,
                stop=stop,
            )

        def by_row(ap):
            return ap.rearrange("p (j c) -> p j c", j=PACK)

        def w2_pass(e, g):
            return w2[e, g * PASS : (g + 1) * PASS, :].rearrange("(p j) n -> p j n", j=PACK)

        offs_list = keep.tile([P, S // PER_COL], U16, name="offs_list")
        pos_lists = [keep.tile([P, T // PER_COL], U16, name="pos_list%d" % r) for r in range(2)]
        tokens = [keep.tile([P, WINDOW], F32, name="tokens%d" % j) for j in range(PACK)]
        gate_first = keep.tile([P, C], F32, name="gate_first")
        gate_rest = keep.tile([P, S - C], F32, name="gate_rest")
        y_front = keep.tile([P, FRONT // P, S], F32, name="y_front")
        y_back = keep.tile([P, S], F32, name="y_back")

        for j in range(PACK):
            nc.gpsimd.memset(tokens[j][:, T:WINDOW], 0.0)

        xT_rows = xT.rearrange("(p j) t -> p j t", j=PACK)
        gate_row = gate.rearrange("(p j) s -> p j s", j=PACK)[:, 0, :]
        nc.sync.dma_start(offs_list[:], offs)
        nc.sync.dma_start(tokens[0][:, 0:T], xT_rows[:, 0, :])
        nc.sync.dma_start(gate_first[:], gate_row[:, 0:C])
        for j in range(1, PACK):
            nc.sync.dma_start(tokens[j][:, 0:T], xT_rows[:, j, :])
        nc.sync.dma_start(gate_rest[:], gate_row[:, C:S])
        w1_raw = []
        for e in range(E):
            w1_raw.append(new("w1_raw%d" % e, PACK * H, F32))
            nc.sync.dma_start(by_row(w1_raw[e][:]), w1[e].rearrange("(p j) i -> p j i", j=PACK))

        w2_whole = new("w2_whole", G * PACK * N, F32)
        whole = [by_row(w2_whole[:, g * PACK * N : (g + 1) * PACK * N]) for g in range(G)]
        for g in range(G):
            nc.sync.dma_start(whole[g], w2_pass(0, g))
        front_raw, back_raw = {}, {}

        def load_w2_part(raw, name, experts, first_col, width, on=None):
            size = PACK * G * width
            held = new(name, len(experts) * size, F32, on)
            for place, e in enumerate(experts):
                raw[e] = by_row(held[:, place * size : (place + 1) * size])
                for g in range(G):
                    src = w2_pass(e, g)[:, :, first_col : first_col + width]
                    nc.sync.dma_start(raw[e][:, :, g * width : (g + 1) * width], src)

        load_w2_part(front_raw, "front_raw1", (1,), 0, FRONT)
        nc.sync.dma_start(pos_lists[0][:], pos1)
        nc.sync.dma_start(pos_lists[1][:], pos2)

        def gather_group(q):
            lo, hi = GROUPS[q][0] * C, (GROUPS[q][-1] + 1) * C
            gathered = new("gathered%d" % q, PACK * (hi - lo), F32)
            for j in range(PACK):
                nc.vector.tensor_tensor(
                    by_row(gathered[:])[:, j, :],
                    tokens[j][:].indirect(offs_list[:, lo // PER_COL : hi // PER_COL]),
                    gate_first[:] if q == 0 else gate_rest[:, lo - C : hi - C],
                    ALU.mult,
                )
            rounded = new("x_bf%d" % q, PACK * (hi - lo), BF16)
            interleave(q in X_ON_SCALAR, rounded[:], by_row(gathered[:]))
            return quantize("x_words%d" % q, rounded, "w1_bf0_1" if q == len(GROUPS) - 1 else None)

        h_words_on = ("w1_bf3_0", "w1_bf3_1", "w1_bf1_0", "h_bf2")
        h_bf, h_words = {}, {}

        def quantize_h(e):
            h_words[e] = quantize("h_words%d" % e, h_bf[e], h_words_on[e])

        x_words = {}
        for e in range(E):
            for q, group in enumerate(GROUPS):
                if e == group[0]:
                    group_words = gather_group(q)
                    for place, member in enumerate(group):
                        x_words[member] = (group_words, place * C)
            halves = []
            for a in range(2):
                halves.append(new("w1_bf%d_%d" % (e, a), 2 * PACK * G * P, BF16))
                copy(
                    (e, a) in W1_ON_SCALAR,
                    halves[a][:].rearrange("p (t m j) -> p m j t", t=2, j=PACK),
                    w1_raw[e][:].rearrange("p (j m t) -> p m j t", j=PACK, t=PACK)[:, :, :, 2 * a : 2 * a + 2],
                )
            if e == 0:
                load_w2_part(front_raw, "front_raw23", (2, 3), 0, FRONT, "w1_raw0")
            if e == 1:
                load_w2_part(back_raw, "back_raw", (1, 2, 3), FRONT, BACK, "w1_raw1")
            w1_words = []
            for a in range(2):
                w1_words.append(quantize("w1_words%d_%d" % (e, a), halves[a]))
                if e == LAST:
                    quantize_h(a)
            for g in range(G):
                relu = new("relu%d_%d" % (e, g), PACK * C, F32, "relu_ring%d" % ((G * e + g) % RELU_RING))
                for s in range(C // P):
                    bank = new_bank("a%d_%d_%d" % (e, g, s), [P, PACK, P])
                    for t in range(PACK):
                        col = (t % 2) * G * P + g * P
                        matmul(bank[:, t, :], w1_words[t // 2], col, x_words[e][0], x_words[e][1] + s * P, P, True, True)
                    nc.scalar.activation(
                        relu[:, s * PASS : (s + 1) * PASS].rearrange("p (n t) -> p n t", t=PACK),
                        bank[:].rearrange("p t n -> p n t"),
                        ACT.Relu,
                    )
                if g == 0:
                    h_bf[e] = new("h_bf%d" % e, G * PACK * C, BF16)
                nc.scalar.activation(h_bf[e][:, g * PACK * C : (g + 1) * PACK * C], relu[:], ACT.Square)

        def second_layer(dst, w2_words, width, block, e):
            for g in range(G):
                matmul(dst, w2_words, g * width + block * P, h_words[e], g * C, C, g == 0, g == G - 1)

        front_bf_on = ("w1_bf0_0", None, "w1_bf1_0", "w1_bf1_1")
        for e in range(E):
            rounded = new("front_bf%d" % e, G * PACK * FRONT, BF16, front_bf_on[e])
            if e in (0, LAST):
                for g in range(G):
                    rows = whole[g][:, :, 0:FRONT] if e == 0 else front_raw[e][:, :, g * FRONT : (g + 1) * FRONT]
                    interleave(False, rounded[:, g * PACK * FRONT : (g + 1) * PACK * FRONT], rows)
            else:
                interleave(False, rounded[:], front_raw[e])
            words = quantize("front_words%d" % e, rounded, "w1_words%d_%d" % divmod(e, 2))
            if e == LAST - 1:
                quantize_h(e)
                quantize_h(LAST)
            slots = slice(e * C, (e + 1) * C)
            if e < LAST:
                bank = new_bank("y_front%d" % e, [P, FRONT // P, C])
                for block in range(FRONT // P):
                    second_layer(bank[:, block, :], words, FRONT, block, e)
                nc.scalar.copy(y_front[:, :, slots], bank[:])
            else:
                for block in range(FRONT // P):
                    bank = new_bank("y_front%d_%d" % (e, block), [P, FRONT // P, C])
                    second_layer(bank[:, block, :], words, FRONT, block, e)
                    nc.scalar.copy(y_front[:, block, slots], bank[:, block, :])

        for e in range(E):
            rounded = new("back_bf%d" % e, G * PACK * BACK, BF16, "x_bf%d" % e if e < len(GROUPS) else None)
            if e == 0:
                for g in range(G):
                    interleave(False, rounded[:, g * PACK * BACK : (g + 1) * PACK * BACK], whole[g][:, :, FRONT:N])
            else:
                interleave(e in BACK_ON_SCALAR, rounded[:], back_raw[e])
            words = quantize("back_words%d" % e, rounded)
            bank = new_bank("y_back%d" % e, [P, C])
            second_layer(bank[:], words, BACK, 0, e)
            nc.scalar.copy(y_back[:, e * C : (e + 1) * C], bank[:])

        def gather_results(picked, window, lo, hi):
            pair = [picked[:, r * T + lo : r * T + hi] for r in range(2)]
            for r in range(2):
                nc.vector.tensor_copy(pair[r], window.indirect(pos_lists[r][:, lo // PER_COL : hi // PER_COL]))
            return pair

        picked_on = ("gathered0", "w1_raw1")
        total_on = ("back_bf%d" % LAST, None)
        for block in range(FRONT // P):
            picked = new("picked%d" % block, 2 * T, F32, picked_on[block])
            first, second = gather_results(picked, y_front[:, block, :], 0, T)
            total = new("total%d" % block, T, F32, total_on[block])
            nc.gpsimd.tensor_add(total[:], first, second)
            nc.sync.dma_start(out[block * P : (block + 1) * P, :], total[:])

        picked = new("picked_back", 2 * T, F32, "gathered%d" % (len(GROUPS) - 1))
        for lo in range(0, T, T // 2):
            first, second = gather_results(picked, y_back[:], lo, lo + T // 2)
            nc.vector.tensor_add(first, first, second)
            nc.sync.dma_start(out[FRONT:N, lo : lo + T // 2], first)
